import numpy as np, ml_dtypes
CORES = [2,6,10,14,18,22,26,30]
N = 8
BF = ml_dtypes.bfloat16
def gentries(a):
    return np.ascontiguousarray(a.reshape(8, 16, -1).transpose(0, 2, 1)).reshape(8, -1)
def gtable(e):
    e = np.asarray(e); return np.ascontiguousarray(e.reshape(8, -1, 16).transpose(0, 2, 1)).reshape(128, -1).astype(np.int32)
def f(rng, *shape):
    return (rng.standard_normal(shape, dtype=np.float32) * np.exp2(rng.integers(-2, 3, shape[:-1] + (1,)))).astype(BF)
def wide(rng, *shape):
    v = f(rng, *shape).astype(np.float32); k = shape[:-2] + (1, shape[-1])
    return (v * np.exp2(rng.integers(-6, 7, k)) * (rng.random(k) > 0.0625)).astype(BF)
M, S, D, Q = 2048, 32, 16, 4
P = N // Q
def forest(rng, L, aside, bushy, zero=False):
    free = S + rng.permutation(M - S); n = S * (D - 1)
    chain = np.concatenate([np.arange(S)[:, None], free[:n].reshape(S, D - 1)], 1)
    p = np.arange(M); dep = np.full(M, -1); dep[chain] = np.arange(D); p[chain[:, 1:]] = chain[:, :-1]; rest = free[n:]
    if bushy:
        h = len(rest) // 2; p[rest[:h]] = rng.integers(0, S); p[rest[h:]] = chain[rng.integers(0, S), D - 2]
    else:
        lev = rng.integers(1, D, len(rest))
        for d in range(1, D):
            v = rest[lev == d]; p[v] = rng.choice(np.flatnonzero(dep == d - 1), len(v)); dep[v] = d
    kids = S + rng.permutation(M - S); o = kids[np.argsort(p[kids], kind="stable")]; q = p[o]
    sib = np.zeros(M, np.int64); sib[o] = np.arange(M - S) - np.searchsorted(q, q); c = np.bincount(q, minlength=M)
    base = rng.integers(0, 4096, M); step = 2 * rng.integers(0, 2048, M) + 1
    if zero: base[0] = 0
    x = np.where((c > 0) & (rng.random(M) < 0.7), (rng.random(M) * c).astype(np.int64), c + (rng.random(M) * (4096 - c)).astype(np.int64))
    x[chain[:, :-1]] = sib[chain[:, 1:]]
    e = np.flatnonzero(L < D - 1); b = chain[e, L[e]]; w = sib[chain[e, L[e] + 1]]; cb = c[b]
    other = (w + 1 + (rng.random(len(e)) * (cb - 1)).astype(np.int64)) % cb; none = cb + (rng.random(len(e)) * (4096 - cb)).astype(np.int64)
    x[b] = np.where((cb > 1) & (rng.random(len(e)) < aside), other, none)
    t = (base + step * x) % 4096
    k = np.zeros(M, np.int64); k[o] = (base[q] + step[q] * sib[o]) % 4096
    k[:S] = np.where(rng.random(S) < 0.5, t[:S], rng.integers(0, 4096, S))
    return p, k, t
def shards(rng, t, sc, tie):
    v = sc * 4096 + t; win = rng.integers(0, N, t.shape); u = rng.random((N,) + t.shape)
    o = np.where(rng.random(t.shape) < tie, sc * 4096 + (u * (t + 1)).astype(np.int64), (u * (v + 1)).astype(np.int64))
    o = np.where((np.arange(N)[:, None, None, None] == win) | (rng.random(o.shape) < 0.03125), v, np.minimum(o, v))
    return np.ascontiguousarray(o.transpose(0, 2, 1, 3)).reshape(N, 8, N * M).astype(np.int32)
def draw(rng, L, aside=0.5, bushy=False, tie=0.125, uneven=False, zero=False):
    a = [[forest(rng, L[q, g], aside, bushy, zero) for g in range(8)] for q in range(N)]
    p, k, t = [np.array([[a[q][g][i] for g in range(8)] for q in range(N)]) for i in range(3)]
    sc = rng.integers(0, 4096, t.shape)
    if uneven: sc = 4095 >> rng.integers(0, 13, t.shape)
    return {"par": np.stack([gtable(p[q]) for q in range(N)]), "tok": k.astype(np.int32), "best": shards(rng, t, sc, tie), "kv": f(rng, N, 128, Q * M)}
def setup_inputs(rng):
    return draw(rng, rng.integers(0, D, (N, 8, S)))
def setup_inputs_full(rng):
    return draw(rng, np.full((N, 8, S), D - 1))
def setup_inputs_cut(rng):
    return draw(rng, rng.choice(np.array([0, 1, D - 2]), (N, 8, S)), aside=0.0, zero=True)
def setup_inputs_ties(rng):
    return draw(rng, rng.integers(0, D, (N, 8, S)), tie=1.0)
def setup_inputs_bushy(rng):
    return draw(rng, rng.integers(0, D, (N, 8, S)), bushy=True)
def setup_inputs_spread(rng):
    d = draw(rng, rng.integers(0, D, (N, 8, S)), uneven=True); d["kv"] = wide(rng, N, 128, Q * M); return d
def check_inputs(d):
    bad = []; p = np.stack([gentries(a) for a in d["par"]]).astype(np.int64); k = d["tok"].astype(np.int64); b = d["best"]
    if not np.isfinite(d["kv"].astype(np.float32)).all(): bad.append("finite")
    if b.min() < 0 or b.max() >= 1 << 24: bad.append("best")
    if k.min() < 0 or k.max() > 4095: bad.append("tokens")
    if p.min() < 0 or p.max() >= M: return bad + ["parents"]
    if (p[:, :, :S] != np.arange(S)).any(): bad.append("roots")
    a = p
    for i in range(D - 2): a = np.take_along_axis(p, a, 2)
    if (a >= S).any(): bad.append("depth")
    w = np.sort((p * 4096 + k)[:, :, S:], axis=2)
    if (w[:, :, 1:] == w[:, :, :-1]).any(): bad.append("children")
    return bad
def reference(par, tok, best, kv):
    p = np.stack([gentries(a) for a in par]).astype(np.int64)
    t = np.max(best, axis=0).reshape(8, N, M).transpose(1, 0, 2) & 4095
    ok = (np.arange(M) < S) | (tok == np.take_along_axis(t, p, 2))
    a = np.broadcast_to(np.arange(M), p.shape); acc = np.ones(p.shape, bool); dep = np.zeros(p.shape, np.int64)
    for i in range(D):
        acc = acc & np.take_along_axis(ok, a, 2); dep = dep + (a >= S); a = np.take_along_axis(p, a, 2)
    y = np.zeros((N, 128, Q * S * D), BF)
    for r in range(N):
        out = y[r].reshape(8, 16, Q * S * D)
        for i in range(Q):
            q = P * i + r % P; k = kv[r][:, i * M:(i + 1) * M].reshape(8, 16, M)
            g, j = np.nonzero(acc[q])
            out[g, :, (i * S + a[q, g, j]) * D + dep[q, g, j]] = k[g, :, j]
    return {"y": y}

@@ -1,0 +1,317 @@
+from concourse.bass import DstId, RemoteDMATransfer
+from concourse.mybir import AluOpType as A, ActivationFunctionType as AF
+
+M, S, D, Q = 2048, 32, 16, 4
+Z = 64
+W = M + Z
+PIECES = [(0, 16), (16, 48), (48, 80), (80, 128)]
+
+SCRATCH = {
+    "dsc": ("dram", [8, 128, 128], "int32"),
+    "land": ("sbuf", [128, 1024], "int32"),
+    "parw": ("sbuf", [128, 128], "int32"),
+    "tokc": ("sbuf", [128, 128], "int32"),
+    "it1": ("sbuf", [128, 128], "int32"),
+    "it2": ("sbuf", [128, 128], "int32"),
+    "acc": ("sbuf", [128, 128], "int32"),
+    "acc2": ("sbuf", [128, 128], "int32"),
+    "tgt": ("sbuf", [128, 128], "int32"),
+    "pcol": ("sbuf", [128, 1], "int32"),
+    "pa": ("sbuf", [128, 1], "int32"),
+    "pg": ("sbuf", [128, 1], "int32"),
+    "cst": ("sbuf", [128, 8], "float32"),
+    "mg": ("sbuf", [128, 128], "float32"),
+    "mb": ("sbuf", [128, 128], "float32"),
+    "bm": ("sbuf", [128, 128], "float32"),
+    "bk2": ("sbuf", [128, 128], "float32"),
+    "bm2": ("sbuf", [128, 128], "float32"),
+    "em": ("sbuf", [128, 2048], "float16"),
+    "fm": ("sbuf", [128, 2048], "bfloat16"),
+    "f32m": ("sbuf", [128, 2048], "float32"),
+    "tokh": ("sbuf", [128, 128], "float16"),
+    "hiw": ("sbuf", [128, 128], "float16"),
+    "lst": ("sbuf", [128, 128], "uint16"),
+    "pars": ("sbuf", [128, 128], "float32"),
+    "ktmp": ("sbuf", [128, 2048], "float32"),
+    "kk": ("sbuf", [128, 2048], "float32"),
+    "eq": ("sbuf", [128, 2048], "bfloat16"),
+    "offt": ("sbuf", [128, 128], "float32"),
+    "offu": ("sbuf", [128, 128], "uint16"),
+    "vals": ("sbuf", [128, 2048], "float32"),
+    "nxt": ("sbuf", [128, W + M], "float32"),
+    "c16": ("sbuf", [128, 128], "bfloat16"),
+    "ones": ("sbuf", [128, 128], "bfloat16"),
+    "colb": ("sbuf", [128, 32], "float32"),
+    "s64": ("sbuf", [128, 32], "float32"),
+    "mask": ("sbuf", [128, 32], "float32"),
+    "res": ("sbuf", [128, 32], "float32"),
+    "md": ("sbuf", [128, 32 * D], "float32"),
+    "sc": ("sbuf", [128, 32 * D], "float32"),
+    "offw": ("sbuf", [128, 2 * D], "uint16"),
+    "lu": ("sbuf", [128, 32], "uint16"),
+    "lists": ("sbuf", [128, 32 * Q], "uint16"),
+    "kvw": ("sbuf", [128, W * Q], "bfloat16"),
+    "ysb": ("sbuf", [128, 512 * Q], "bfloat16"),
+    "psA": ("psum", [128, 2048], "float32"),
+    "psB": ("psum", [128, 2048], "float32"),
+}
+SEMAPHORES = ["vs", "ss", "ps", "gs", "ldD", "ldS", "ldM", "ldP", "ldO", "ldpar", "ldtok", "ldkv", "sent", "aD", "aS", "aM",
+              "aP", "lsent", "li0", "li1", "li2", "li3", "stored"]
+
+
+def rank_program(g, core, T, topo):
+    rank = T.rank_of(core)
+    if rank is None:
+        return
+    eng = {"v": g.vector, "s": g.scalar, "p": g.tensor, "g": g, "y": g.sync}
+    semof = {"v": "vs", "s": "ss", "p": "ps", "g": "gs"}
+    count = {"v": 0, "s": 0, "p": 0, "g": 0}
+    seen = {}
+
+    def need(q, deps):
+        for name, val in deps:
+            if seen.get((q, name), 0) < val:
+                eng[q].wait_ge(T.sem[name], int(val))
+                seen[(q, name)] = val
+
+    def done(q, ins):
+        count[q] += 1
+        ins.then_inc(T.sem[semof[q]], 1)
+        return (semof[q], count[q])
+
+    chip = topo.chip(core)
+    same, mate, plane, diag = [], [], [], []
+    for c in T.cores:
+        if c == core:
+            continue
+        oc = topo.chip(c)
+        if oc == chip:
+            same.append(c)
+        elif topo.mates(chip, oc):
+            mate.append(c)
+        elif topo.same_plane(chip, oc):
+            plane.append(c)
+        else:
+            diag.append(c)
+    off = topo.engines(core, diag[0])
+    half = len(off) // 2
+    bits = lambda es: sum(1 << e for e in es)
+    inner = [e for e in topo.engines(core, same[0]) if e not in off]
+
+    def dst_id(c):
+        a = topo.addr(c)
+        return DstId(rid=a[0], pnc=a[1])
+
+    slot = lambda r: T.land[:, r * 128:(r + 1) * 128]
+    piece = lambda r: T.best[:, r * M:(r + 1) * M]
+    R = T.rank_of
+
+    for grp, sem in ((diag, "ldD"), (plane, "ldS")):
+        for c in grp:
+            g.sync.dma_start(T.dsc[R(c)], piece(R(c))).then_inc(T.sem[sem], 16)
+    g.scalar.dma_start(T.parw[:], T.par[:]).then_inc(T.sem.ldpar, 16)
+    g.scalar.dma_start(T.tokc[:], T.tok[:]).then_inc(T.sem.ldtok, 16)
+    for c in mate:
+        g.scalar.dma_start(T.dsc[R(c)], piece(R(c))).then_inc(T.sem.ldM, 16)
+    g.scalar.dma_start(T.dsc[R(same[0])], piece(R(same[0]))).then_inc(T.sem.ldP, 16)
+    g.scalar.dma_start(slot(rank), piece(rank)).then_inc(T.sem.ldO, 16)
+
+    i_p = done("g", g.iota(T.pcol[:], [[1, 1]], 0, 1))
+    i_mg = done("g", g.iota(T.mg[:], [[1, 8], [0, 16]], 0, 0, allow_small_or_imprecise_dtypes=True))
+    i_mb = done("g", g.iota(T.mb[:], [[0, 8], [1, 16]], 0, 0, allow_small_or_imprecise_dtypes=True))
+    for grp, ld, ar in ((diag, "ldD", "aD"), (plane, "ldS", "aS"), (mate, "ldM", "aM")):
+        need("g", [(ld, 32)])
+        g.remote_dma_fused([RemoteDMATransfer(dst_ids=[dst_id(c)], dma_engine_mask=bits(off[k * half:(k + 1) * half]),
+                                              remote_sem=T.sem[ar], src=T.dsc[R(c)], dst=slot(rank))
+                            for k, c in enumerate(grp)], local_sem=T.sem.sent)
+    need("g", [("ldP", 16)])
+    g.remote_dma_fused([RemoteDMATransfer(dst_ids=[dst_id(same[0])], dma_engine_mask=bits(inner),
+                                          remote_sem=T.sem.aP, src=T.dsc[R(same[0])], dst=slot(rank))],
+                       local_sem=T.sem.sent)
+    i_c16 = done("g", g.iota(T.c16[:], [[16, 128]], 0, 0, allow_small_or_imprecise_dtypes=True))
+    i_cb = done("g", g.iota(T.colb[:], [[0, 2], [1, 16]], 0, 0, allow_small_or_imprecise_dtypes=True))
+    i_s64 = done("g", g.iota(T.s64[:], [[1, 32]], Z, 0, allow_small_or_imprecise_dtypes=True))
+    i_val = done("g", g.iota(T.vals[:], [[1, M]], Z, 0, allow_small_or_imprecise_dtypes=True))
+
+    need("y", [("sent", 3 * len(off) + len(inner))])
+    for i in range(Q):
+        g.sync.dma_start(T.kvw[:, i * W + Z:(i + 1) * W], T.kv[:, i * M:(i + 1) * M]).then_inc(T.sem.ldkv, 16)
+
+    v, t, s = g.vector, g.tensor, g.scalar
+    col = lambda k: T.cst[:, k:k + 1]
+
+    need("v", [i_p])
+    a = done("v", v.tensor_scalar(T.pa[:], T.pcol[:], 15, None, A.bitwise_and))
+    b = done("v", v.tensor_scalar(T.pg[:], T.pcol[:], 4, None, A.arith_shift_right))
+    need("v", [b])
+    c0 = done("v", v.tensor_copy(col(2), T.pg[:]))
+    done("v", v.tensor_copy(col(0), T.pa[:]))
+    c1 = done("v", v.tensor_scalar(col(1), T.pa[:], 1.0, None, A.add))
+    need("v", [c1, i_mg])
+    x = done("v", v.tensor_scalar(T.bm[:], T.mg[:], col(2), None, A.is_equal))
+    need("v", [x])
+    x = done("v", v.tensor_scalar(T.bk2[:], T.bm[:], col(1), None, A.mult))
+    need("v", [("ldtok", 16)])
+    done("v", v.tensor_scalar(T.tokh[:], T.tokc[:], -2048.0, None, A.add))
+    need("v", [x])
+    ems = [done("v", v.tensor_scalar(T.em[:, k * 128:(k + 1) * 128], T.bk2[:], float(k + 1), None, A.is_equal)) for k in range(16)]
+    need("v", [("ldpar", 16)])
+    x1 = done("v", v.tensor_scalar(T.it1[:], T.parw[:], 1920, None, A.bitwise_and))
+    x2 = done("v", v.tensor_scalar(T.it2[:], T.parw[:], 127, None, A.bitwise_and))
+    kb = done("v", v.tensor_scalar(col(3), col(0), -4096.0, 2048.0, A.mult, A.add))
+    need("v", [x1])
+    v_hi = done("v", v.tensor_scalar(T.hiw[:], T.it1[:], 32.0, None, A.mult))
+    need("v", [x2])
+    v_lst = done("v", v.tensor_copy(T.lst[:], T.it2[:]))
+    v_c4 = done("v", v.tensor_scalar(col(4), col(0), float(W), None, A.add))
+    v_pars = done("v", v.tensor_scalar(T.pars[:], T.parw[:], col(0), -2048.0, A.subtract, A.add))
+    need("v", [i_mb])
+    x = done("v", v.tensor_scalar(T.mb[:], T.mb[:], 1.0, None, A.add))
+    need("v", [x])
+    x = done("v", v.tensor_tensor(T.bm2[:], T.bm[:], T.mb[:], A.mult))
+    v_ones = done("v", v.memset(T.ones[:], 1.0 / 128))
+    need("v", [x])
+    for k in range(16):
+        v_f = done("v", v.tensor_scalar(T.fm[:, k * 128:(k + 1) * 128], T.bm2[:], float(k + 1), -8192.0, A.is_equal, A.mult))
+
+    pa_done, pb_done = [], []
+    for bank in range(4):
+        for k in range(4 * bank, 4 * bank + 4):
+            need("p", [ems[k]])
+            ins = t.matmul(T.psA[:, k * 128:(k + 1) * 128], T.em[:, k * 128:(k + 1) * 128], T.tokh[:], True, True)
+        pa_done.append(done("p", ins))
+    need("p", [v_hi])
+    for bank in range(4):
+        for k in range(16):
+            ins = t.matmul(T.psB[:, bank * 512 + k:(bank + 1) * 512:16], T.em[:, k * 128:(k + 1) * 128],
+                           T.hiw[:, bank * 32:(bank + 1) * 32], True, True)
+        pb_done.append(done("p", ins))
+
+    need("s", [kb])
+    ks = []
+    for bank in range(4):
+        need("s", [pa_done[bank]])
+        cs = slice(bank * 512, (bank + 1) * 512)
+        ks.append(done("s", s.activation(T.ktmp[:, cs], T.psA[:, cs], AF.Identity, bias=col(3), scale=1.0)))
+    s_z1 = done("s", s.activation(T.nxt[:, Z:W], T.ktmp[:], AF.Silu, scale=0.0)) if False else None
+    need("s", [ks[3]])
+    done("s", s.activation(T.nxt[:, 0:M], T.ktmp[:], AF.Silu, scale=0.0))
+    s_zero = done("s", s.activation(T.nxt[:, M:W], T.ktmp[:, 0:Z], AF.Silu, scale=0.0))
+    need("s", [v_f])
+    s_f32 = done("s", s.activation(T.f32m[:], T.fm[:], AF.Copy, scale=-1.0 / 8192))
+    vk = []
+    for bank in range(4):
+        need("v", [ks[bank], pb_done[bank]])
+        cs = slice(bank * 512, (bank + 1) * 512)
+        vk.append(done("v", v.tensor_tensor(T.kk[:, cs], T.psB[:, cs], T.ktmp[:, cs], A.add)))
+    need("v", [vk[0]])
+    v_k = done("v", v.memset(T.kk[:, 0:S], -1.0))
+    for i in range(Q):
+        v_kz = done("v", v.memset(T.kvw[:, i * W:i * W + Z], 0.0))
+    need("v", [i_s64])
+    x = done("v", v.tensor_scalar(T.mask[:], T.colb[:], col(0), 1.0 + 2.0 ** -13, A.is_equal, A.mult))
+    y1 = done("v", v.memset(T.res[:], 1.0))
+    for k in range(2):
+        v_o0 = done("v", v.tensor_scalar(T.offw[:, k:k + 1], col(0), float(Z + 16 * k), None, A.add))
+    need("v", [y1])
+    v_res = done("v", v.memset(T.res[:, 16:17], 0.0))
+    v_m0 = done("v", v.tensor_tensor(T.md[:, 0:32], T.mask[:], T.s64[:], A.mult))
+
+    need("p", [v_ones, i_c16])
+    for n, (ca, cb) in enumerate(PIECES):
+        need("p", [ks[n]])
+        t.matmul(T.psA[:, n * 512:n * 512 + cb - ca], T.ones[:], T.c16[:, ca:cb], True, False)
+
+    m = lambda o, p, q: done("v", v.tensor_tensor(o, p, q, A.max))
+    need("v", [("ldO", 16), ("aD", 2 * half)])
+    x = m(T.acc[:], slot(R(diag[0])), slot(R(diag[1])))
+    need("v", [x])
+    x = m(T.acc[:], T.acc[:], slot(rank))
+    need("v", [("aS", 2 * half)])
+    z = m(T.acc2[:], slot(R(plane[0])), slot(R(plane[1])))
+    need("v", [z])
+    x = m(T.acc[:], T.acc[:], T.acc2[:])
+    need("v", [x, ("aP", len(inner))])
+    x = m(T.acc[:], T.acc[:], slot(R(same[0])))
+    need("v", [("aM", 2 * half)])
+    z = m(T.acc2[:], slot(R(mate[0])), slot(R(mate[1])))
+    need("v", [z])
+    x = m(T.acc[:], T.acc[:], T.acc2[:])
+    need("v", [x])
+    x = done("v", v.tensor_scalar(T.tgt[:], T.acc[:], 4095, None, A.bitwise_and))
+    need("v", [x, v_k])
+
+    v_eq, p_ok = [], []
+
+    def fit(n):
+        ca, cb = PIECES[n]
+        e = done("v", v.tensor_tensor(T.eq[:, 16 * ca:16 * cb], T.tgt[:].indirect(T.lst[:, ca:cb]), T.kk[:, 16 * ca:16 * cb], A.is_equal))
+        need("p", [e])
+        for k in range(16):
+            ins = t.matmul(T.psA[:, n * 512:n * 512 + cb - ca], T.fm[:, k * 128:(k + 1) * 128], T.eq[:, 16 * ca + k:16 * cb:16],
+                           False, k == 15)
+        p_ok.append(done("p", ins))
+
+    scat = []
+
+    def place(n):
+        ca, cb = PIECES[n]
+        need("v", [p_ok[n]])
+        o = done("v", v.tensor_tensor(T.offt[:, ca:cb], T.psA[:, n * 512:n * 512 + cb - ca], T.pars[:, ca:cb], A.max))
+        need("v", [o])
+        o = done("v", v.tensor_scalar(T.offu[:, ca:cb], T.offt[:, ca:cb], col(4), None, A.add))
+        need("s", [o, i_val, scat[-1] if scat else s_f32])
+        scat.append(done("s", s.activation(T.nxt[:].indirect(T.offu[:, ca:cb]), T.vals[:, 16 * ca:16 * cb], AF.Silu)))
+
+    fit(0)
+    fit(1)
+    place(0)
+    fit(2)
+    place(1)
+    fit(3)
+    place(2)
+    place(3)
+
+    def collect(d, dep):
+        need("p", [dep, s_f32, vk[0]])
+        ins = t.matmul(T.psB[:, 0:32], T.f32m[:, d * 128:(d + 1) * 128], T.md[:, 32 * d:32 * d + 32], d == 0, d == D - 1)
+        return done("p", ins) if d == D - 1 else None
+
+    collect(0, v_m0)
+    need("v", [scat[-1]])
+    for d in range(1, D):
+        x = done("v", v.tensor_tensor(T.md[:, 32 * d:32 * d + 32], T.nxt[:, 0:W].indirect(T.offw[:, 2 * d - 2:2 * d]), T.mask[:], A.mult))
+        p_l = collect(d, x)
+        if d < D - 1:
+            need("v", [x])
+            x = done("v", v.tensor_tensor_scan(T.sc[:, 32 * d:32 * d + 32], T.res[:], T.md[:, 32 * d:32 * d + 32], 0.0, A.mult, A.add))
+            need("v", [x])
+            x = done("v", v.tensor_copy(T.offw[:, 2 * d:2 * d + 2], T.sc[:, 32 * d + 15:32 * d + 32:16]))
+            need("v", [x])
+    need("v", [p_l])
+    v_lu = done("v", v.tensor_copy(T.lu[:], T.psB[:, 0:32]))
+
+    me = rank // 2
+    heads = [c for c in diag + plane + mate if R(c) % 2 == rank % 2]
+    need("g", [v_lu])
+    mine = T.lists[:, me * 32:(me + 1) * 32]
+    g.remote_dma_fused([RemoteDMATransfer(dst_ids=[dst_id(c) for c in heads], dma_engine_mask=bits(off), remote_sem=T.sem["li%d" % me],
+                                          srcs=[T.lu[:]], dsts=[mine for c in heads], alu_op=0)], local_sem=T.sem.lsent)
+
+    order = [None] + [c for c in mate + plane + diag if c in heads]
+    need("v", [("ldkv", 16 * Q), v_lu])
+    need("s", [("ldkv", 16 * Q), v_lu])
+    for n, c in enumerate(order):
+        i = me if c is None else R(c) // 2
+        win = T.kvw[:, i * W:(i + 1) * W]
+        src = T.lu if c is None else T.lists
+        b0 = 0 if c is None else 32 * i
+        if c is not None:
+            need("v", [("li%d" % i, len(off))])
+            need("s", [("li%d" % i, len(off))])
+        e1 = done("v", v.tensor_copy(T.ysb[:, i * 512:i * 512 + 256], win.indirect(src[:, b0:b0 + 16])))
+        e2 = done("s", s.activation(T.ysb[:, i * 512 + 256:(i + 1) * 512], win.indirect(src[:, b0 + 16:b0 + 32]), AF.Copy))
+        need("y", [e1, e2])
+        g.sync.dma_start(T.y[:, i * 512:(i + 1) * 512], T.ysb[:, i * 512:(i + 1) * 512]).then_inc(T.sem.stored, 16)
+    need("g", [("lsent", len(off)), ("gs", count["g"]), ("ps", count["p"])])
+    need("y", [("stored", 16 * Q)])

@@ -4,7 +4,7 @@ from concourse.mybir import AluOpType as A, ActivationFunctionType as AF
 M, S, D, Q = 2048, 32, 16, 4
 Z = 64
 W = M + Z
-PIECES = [(0, 16), (16, 48), (48, 80), (80, 128)]
+PIECES = [(2, 16), (16, 48), (48, 80), (80, 128)]
 
 SCRATCH = {
     "dsc": ("dram", [8, 128, 128], "int32"),
@@ -22,9 +22,9 @@ SCRATCH = {
     "cst": ("sbuf", [128, 8], "float32"),
     "mg": ("sbuf", [128, 128], "float32"),
     "mb": ("sbuf", [128, 128], "float32"),
-    "bm": ("sbuf", [128, 128], "float32"),
-    "bk2": ("sbuf", [128, 128], "float32"),
-    "bm2": ("sbuf", [128, 128], "float32"),
+    "bm": ("sbuf", [128, 128], "float16"),
+    "bk2": ("sbuf", [128, 128], "float16"),
+    "bm2": ("sbuf", [128, 128], "bfloat16"),
     "em": ("sbuf", [128, 2048], "float16"),
     "fm": ("sbuf", [128, 2048], "bfloat16"),
     "f32m": ("sbuf", [128, 2048], "float32"),
@@ -41,8 +41,6 @@ SCRATCH = {
     "nxt": ("sbuf", [128, W + M], "float32"),
     "c16": ("sbuf", [128, 128], "bfloat16"),
     "ones": ("sbuf", [128, 128], "bfloat16"),
-    "colb": ("sbuf", [128, 32], "float32"),
-    "s64": ("sbuf", [128, 32], "float32"),
     "mask": ("sbuf", [128, 32], "float32"),
     "res": ("sbuf", [128, 32], "float32"),
     "md": ("sbuf", [128, 32 * D], "float32"),
@@ -104,21 +102,23 @@ def rank_program(g, core, T, topo):
 
     slot = lambda r: T.land[:, r * 128:(r + 1) * 128]
     piece = lambda r: T.best[:, r * M:(r + 1) * M]
+    blk = lambda k: slice(k * 128, (k + 1) * 128)
     R = T.rank_of
 
     for grp, sem in ((diag, "ldD"), (plane, "ldS")):
         for c in grp:
             g.sync.dma_start(T.dsc[R(c)], piece(R(c))).then_inc(T.sem[sem], 16)
-    g.scalar.dma_start(T.parw[:], T.par[:]).then_inc(T.sem.ldpar, 16)
     g.scalar.dma_start(T.tokc[:], T.tok[:]).then_inc(T.sem.ldtok, 16)
+    g.scalar.dma_start(T.parw[:], T.par[:]).then_inc(T.sem.ldpar, 16)
     for c in mate:
         g.scalar.dma_start(T.dsc[R(c)], piece(R(c))).then_inc(T.sem.ldM, 16)
     g.scalar.dma_start(T.dsc[R(same[0])], piece(R(same[0]))).then_inc(T.sem.ldP, 16)
     g.scalar.dma_start(slot(rank), piece(rank)).then_inc(T.sem.ldO, 16)
 
+    loose = dict(allow_small_or_imprecise_dtypes=True)
     i_p = done("g", g.iota(T.pcol[:], [[1, 1]], 0, 1))
-    i_mg = done("g", g.iota(T.mg[:], [[1, 8], [0, 16]], 0, 0, allow_small_or_imprecise_dtypes=True))
-    i_mb = done("g", g.iota(T.mb[:], [[0, 8], [1, 16]], 0, 0, allow_small_or_imprecise_dtypes=True))
+    i_mg = done("g", g.iota(T.mg[:], [[1, 8], [0, 16]], 0, 0, **loose))
+    i_mb = done("g", g.iota(T.mb[:], [[0, 8], [1, 16]], 1, 0, **loose))
     for grp, ld, ar in ((diag, "ldD", "aD"), (plane, "ldS", "aS"), (mate, "ldM", "aM")):
         need("g", [(ld, 32)])
         g.remote_dma_fused([RemoteDMATransfer(dst_ids=[dst_id(c)], dma_engine_mask=bits(off[k * half:(k + 1) * half]),
@@ -128,10 +128,11 @@ def rank_program(g, core, T, topo):
     g.remote_dma_fused([RemoteDMATransfer(dst_ids=[dst_id(same[0])], dma_engine_mask=bits(inner),
                                           remote_sem=T.sem.aP, src=T.dsc[R(same[0])], dst=slot(rank))],
                        local_sem=T.sem.sent)
-    i_c16 = done("g", g.iota(T.c16[:], [[16, 128]], 0, 0, allow_small_or_imprecise_dtypes=True))
-    i_cb = done("g", g.iota(T.colb[:], [[0, 2], [1, 16]], 0, 0, allow_small_or_imprecise_dtypes=True))
-    i_s64 = done("g", g.iota(T.s64[:], [[1, 32]], Z, 0, allow_small_or_imprecise_dtypes=True))
-    i_val = done("g", g.iota(T.vals[:], [[1, M]], Z, 0, allow_small_or_imprecise_dtypes=True))
+    i_c16 = done("g", g.iota(T.c16[:], [[16, 128]], 0, 0, **loose))
+    i_val = []
+    for n, (ca, cb) in enumerate(PIECES):
+        j = 16 * ca if n else 0
+        i_val.append(done("g", g.iota(T.vals[:, j:16 * cb], [[1, 16 * cb - j]], Z + j, 0, **loose)))
 
     need("y", [("sent", 3 * len(off) + len(inner))])
     for i in range(Q):
@@ -141,50 +142,55 @@ def rank_program(g, core, T, topo):
     col = lambda k: T.cst[:, k:k + 1]
 
     need("v", [i_p])
-    a = done("v", v.tensor_scalar(T.pa[:], T.pcol[:], 15, None, A.bitwise_and))
     b = done("v", v.tensor_scalar(T.pg[:], T.pcol[:], 4, None, A.arith_shift_right))
+    a = done("v", v.tensor_scalar(T.pa[:], T.pcol[:], 15, None, A.bitwise_and))
     need("v", [b])
     c0 = done("v", v.tensor_copy(col(2), T.pg[:]))
+    need("v", [a])
+    done("v", v.tensor_scalar(col(1), T.pa[:], 1.0, None, A.add))
     done("v", v.tensor_copy(col(0), T.pa[:]))
-    c1 = done("v", v.tensor_scalar(col(1), T.pa[:], 1.0, None, A.add))
-    need("v", [c1, i_mg])
+    need("v", [c0, i_mg])
     x = done("v", v.tensor_scalar(T.bm[:], T.mg[:], col(2), None, A.is_equal))
     need("v", [x])
     x = done("v", v.tensor_scalar(T.bk2[:], T.bm[:], col(1), None, A.mult))
-    need("v", [("ldtok", 16)])
-    done("v", v.tensor_scalar(T.tokh[:], T.tokc[:], -2048.0, None, A.add))
+    kb = done("v", v.tensor_scalar(col(3), col(0), -4096.0, 2048.0, A.mult, A.add))
+    v_c4 = done("v", v.tensor_scalar(col(4), col(0), float(W), None, A.add))
+    y1 = done("v", v.memset(T.res[:], 1.0))
     need("v", [x])
-    ems = [done("v", v.tensor_scalar(T.em[:, k * 128:(k + 1) * 128], T.bk2[:], float(k + 1), None, A.is_equal)) for k in range(16)]
+    ems = [done("v", v.tensor_scalar(T.em[:, blk(k)], T.bk2[:], float(k + 1), None, A.is_equal)) for k in range(16)]
+    need("v", [("ldtok", 16)])
+    v_tok = done("v", v.tensor_scalar(T.tokh[:], T.tokc[:], -2048.0, None, A.add))
     need("v", [("ldpar", 16)])
     x1 = done("v", v.tensor_scalar(T.it1[:], T.parw[:], 1920, None, A.bitwise_and))
     x2 = done("v", v.tensor_scalar(T.it2[:], T.parw[:], 127, None, A.bitwise_and))
-    kb = done("v", v.tensor_scalar(col(3), col(0), -4096.0, 2048.0, A.mult, A.add))
     need("v", [x1])
     v_hi = done("v", v.tensor_scalar(T.hiw[:], T.it1[:], 32.0, None, A.mult))
     need("v", [x2])
     v_lst = done("v", v.tensor_copy(T.lst[:], T.it2[:]))
-    v_c4 = done("v", v.tensor_scalar(col(4), col(0), float(W), None, A.add))
     v_pars = done("v", v.tensor_scalar(T.pars[:], T.parw[:], col(0), -2048.0, A.subtract, A.add))
     need("v", [i_mb])
-    x = done("v", v.tensor_scalar(T.mb[:], T.mb[:], 1.0, None, A.add))
-    need("v", [x])
     x = done("v", v.tensor_tensor(T.bm2[:], T.bm[:], T.mb[:], A.mult))
     v_ones = done("v", v.memset(T.ones[:], 1.0 / 128))
-    need("v", [x])
+    need("v", [x, y1])
     for k in range(16):
-        v_f = done("v", v.tensor_scalar(T.fm[:, k * 128:(k + 1) * 128], T.bm2[:], float(k + 1), -8192.0, A.is_equal, A.mult))
+        v_f = done("v", v.tensor_scalar(T.fm[:, blk(k)], T.bm2[:], float(k + 1), -8192.0, A.is_equal, A.mult))
+    v_mask = done("v", v.tensor_scalar(T.mask[:], T.mb[:, 0:32], col(1), 1.0 + 2.0 ** -13, A.is_equal, A.mult))
+    v_res = done("v", v.memset(T.res[:, 16:17], 0.0))
+    for k in range(2):
+        v_o0 = done("v", v.tensor_scalar(T.offw[:, k:k + 1], col(0), float(Z + 16 * k), None, A.add))
+    for i in range(Q):
+        v_kz = done("v", v.memset(T.kvw[:, i * W:i * W + Z], 0.0))
 
     pa_done, pb_done = [], []
+    need("p", [v_tok])
     for bank in range(4):
         for k in range(4 * bank, 4 * bank + 4):
-            need("p", [ems[k]])
-            ins = t.matmul(T.psA[:, k * 128:(k + 1) * 128], T.em[:, k * 128:(k + 1) * 128], T.tokh[:], True, True)
+            ins = t.matmul(T.psA[:, blk(k)], T.em[:, blk(k)], T.tokh[:], True, True)
         pa_done.append(done("p", ins))
     need("p", [v_hi])
     for bank in range(4):
-        for k in range(16):
-            ins = t.matmul(T.psB[:, bank * 512 + k:(bank + 1) * 512:16], T.em[:, k * 128:(k + 1) * 128],
-                           T.hiw[:, bank * 32:(bank + 1) * 32], True, True)
+        for k in range(4 * bank, 4 * bank + 4):
+            ins = t.matmul(T.psB[:, blk(k)], T.em[:, blk(k)], T.hiw[:], True, True)
         pb_done.append(done("p", ins))
 
     need("s", [kb])
@@ -193,33 +199,16 @@ def rank_program(g, core, T, topo):
         need("s", [pa_done[bank]])
         cs = slice(bank * 512, (bank + 1) * 512)
         ks.append(done("s", s.activation(T.ktmp[:, cs], T.psA[:, cs], AF.Identity, bias=col(3), scale=1.0)))
-    s_z1 = done("s", s.activation(T.nxt[:, Z:W], T.ktmp[:], AF.Silu, scale=0.0)) if False else None
+    need("v", [ks[3]])
+    for k in range(16):
+        need("v", [pb_done[k // 4]])
+        v_k = done("v", v.tensor_tensor(T.kk[:, k:M:16], T.psB[:, blk(k)], T.ktmp[:, k:M:16], A.add))
     need("s", [ks[3]])
     done("s", s.activation(T.nxt[:, 0:M], T.ktmp[:], AF.Silu, scale=0.0))
     s_zero = done("s", s.activation(T.nxt[:, M:W], T.ktmp[:, 0:Z], AF.Silu, scale=0.0))
-    need("s", [v_f])
-    s_f32 = done("s", s.activation(T.f32m[:], T.fm[:], AF.Copy, scale=-1.0 / 8192))
-    vk = []
-    for bank in range(4):
-        need("v", [ks[bank], pb_done[bank]])
-        cs = slice(bank * 512, (bank + 1) * 512)
-        vk.append(done("v", v.tensor_tensor(T.kk[:, cs], T.psB[:, cs], T.ktmp[:, cs], A.add)))
-    need("v", [vk[0]])
-    v_k = done("v", v.memset(T.kk[:, 0:S], -1.0))
-    for i in range(Q):
-        v_kz = done("v", v.memset(T.kvw[:, i * W:i * W + Z], 0.0))
-    need("v", [i_s64])
-    x = done("v", v.tensor_scalar(T.mask[:], T.colb[:], col(0), 1.0 + 2.0 ** -13, A.is_equal, A.mult))
-    y1 = done("v", v.memset(T.res[:], 1.0))
-    for k in range(2):
-        v_o0 = done("v", v.tensor_scalar(T.offw[:, k:k + 1], col(0), float(Z + 16 * k), None, A.add))
-    need("v", [y1])
-    v_res = done("v", v.memset(T.res[:, 16:17], 0.0))
-    v_m0 = done("v", v.tensor_tensor(T.md[:, 0:32], T.mask[:], T.s64[:], A.mult))
 
-    need("p", [v_ones, i_c16])
+    need("p", [v_ones, i_c16, ks[3]])
     for n, (ca, cb) in enumerate(PIECES):
-        need("p", [ks[n]])
         t.matmul(T.psA[:, n * 512:n * 512 + cb - ca], T.ones[:], T.c16[:, ca:cb], True, False)
 
     m = lambda o, p, q: done("v", v.tensor_tensor(o, p, q, A.max))
@@ -241,15 +230,14 @@ def rank_program(g, core, T, topo):
     x = done("v", v.tensor_scalar(T.tgt[:], T.acc[:], 4095, None, A.bitwise_and))
     need("v", [x, v_k])
 
-    v_eq, p_ok = [], []
+    p_ok = []
 
     def fit(n):
         ca, cb = PIECES[n]
         e = done("v", v.tensor_tensor(T.eq[:, 16 * ca:16 * cb], T.tgt[:].indirect(T.lst[:, ca:cb]), T.kk[:, 16 * ca:16 * cb], A.is_equal))
         need("p", [e])
         for k in range(16):
-            ins = t.matmul(T.psA[:, n * 512:n * 512 + cb - ca], T.fm[:, k * 128:(k + 1) * 128], T.eq[:, 16 * ca + k:16 * cb:16],
-                           False, k == 15)
+            ins = t.matmul(T.psA[:, n * 512:n * 512 + cb - ca], T.fm[:, blk(k)], T.eq[:, 16 * ca + k:16 * cb:16], False, k == 15)
         p_ok.append(done("p", ins))
 
     scat = []
@@ -260,7 +248,7 @@ def rank_program(g, core, T, topo):
         o = done("v", v.tensor_tensor(T.offt[:, ca:cb], T.psA[:, n * 512:n * 512 + cb - ca], T.pars[:, ca:cb], A.max))
         need("v", [o])
         o = done("v", v.tensor_scalar(T.offu[:, ca:cb], T.offt[:, ca:cb], col(4), None, A.add))
-        need("s", [o, i_val, scat[-1] if scat else s_f32])
+        need("s", [o, i_val[n], scat[-1] if scat else s_zero])
         scat.append(done("s", s.activation(T.nxt[:].indirect(T.offu[:, ca:cb]), T.vals[:, 16 * ca:16 * cb], AF.Silu)))
 
     fit(0)
@@ -272,9 +260,14 @@ def rank_program(g, core, T, topo):
     place(2)
     place(3)
 
+    need("s", [v_f])
+    s_f32 = done("s", s.activation(T.f32m[:], T.fm[:], AF.Copy, scale=-1.0 / 8192))
+    need("v", [i_val[0], v_mask])
+    v_m0 = done("v", v.tensor_tensor(T.md[:, 0:32], T.mask[:], T.vals[:, 0:32], A.mult))
+
     def collect(d, dep):
-        need("p", [dep, s_f32, vk[0]])
-        ins = t.matmul(T.psB[:, 0:32], T.f32m[:, d * 128:(d + 1) * 128], T.md[:, 32 * d:32 * d + 32], d == 0, d == D - 1)
+        need("p", [dep, s_f32, v_k])
+        ins = t.matmul(T.psB[:, 0:32], T.f32m[:, blk(d)], T.md[:, 32 * d:32 * d + 32], d == 0, d == D - 1)
         return done("p", ins) if d == D - 1 else None
 
     collect(0, v_m0)

@@ -19,15 +19,15 @@ SCRATCH = {
     "pcol": ("sbuf", [128, 1], "int32"),
     "pa": ("sbuf", [128, 1], "int32"),
     "pg": ("sbuf", [128, 1], "int32"),
-    "cst": ("sbuf", [128, 8], "float32"),
+    "cst": ("sbuf", [128, 16], "float32"),
     "mg": ("sbuf", [128, 128], "float32"),
-    "mb": ("sbuf", [128, 128], "float32"),
+    "strip": ("sbuf", [128, 144], "float32"),
+    "step": ("sbuf", [128, 32], "float32"),
     "bm": ("sbuf", [128, 128], "float16"),
     "bk2": ("sbuf", [128, 128], "float16"),
-    "bm2": ("sbuf", [128, 128], "bfloat16"),
     "em": ("sbuf", [128, 2048], "float16"),
-    "fm": ("sbuf", [128, 2048], "bfloat16"),
-    "f32m": ("sbuf", [128, 2048], "float32"),
+    "fm": ("sbuf", [128, 144], "bfloat16"),
+    "f32m": ("sbuf", [128, 144], "float32"),
     "tokh": ("sbuf", [128, 128], "float16"),
     "hiw": ("sbuf", [128, 128], "float16"),
     "lst": ("sbuf", [128, 128], "uint16"),
@@ -42,10 +42,9 @@ SCRATCH = {
     "c16": ("sbuf", [128, 128], "bfloat16"),
     "ones": ("sbuf", [128, 128], "bfloat16"),
     "mask": ("sbuf", [128, 32], "float32"),
-    "res": ("sbuf", [128, 32], "float32"),
+    "res": ("sbuf", [128, 16], "float32"),
     "md": ("sbuf", [128, 32 * D], "float32"),
-    "sc": ("sbuf", [128, 32 * D], "float32"),
-    "offw": ("sbuf", [128, 2 * D], "uint16"),
+    "offw": ("sbuf", [128, 32 * D], "uint16"),
     "lu": ("sbuf", [128, 32], "uint16"),
     "lists": ("sbuf", [128, 32 * Q], "uint16"),
     "kvw": ("sbuf", [128, W * Q], "bfloat16"),
@@ -53,8 +52,8 @@ SCRATCH = {
     "psA": ("psum", [128, 2048], "float32"),
     "psB": ("psum", [128, 2048], "float32"),
 }
-SEMAPHORES = ["vs", "ss", "ps", "gs", "ldD", "ldS", "ldM", "ldP", "ldO", "ldpar", "ldtok", "ldkv", "sent", "aD", "aS", "aM",
-              "aP", "lsent", "li0", "li1", "li2", "li3", "stored"]
+SEMAPHORES = ["vs", "ss", "ps", "gs", "ldD", "ldS", "ldM", "ldP", "ldO", "ldpar", "ldtok", "ldk0", "ldk1", "ldk2", "ldk3",
+              "sent", "aD", "aS", "aM", "aP", "lsent", "li0", "li1", "li2", "li3", "stored"]
 
 
 def rank_program(g, core, T, topo):
@@ -118,7 +117,7 @@ def rank_program(g, core, T, topo):
     loose = dict(allow_small_or_imprecise_dtypes=True)
     i_p = done("g", g.iota(T.pcol[:], [[1, 1]], 0, 1))
     i_mg = done("g", g.iota(T.mg[:], [[1, 8], [0, 16]], 0, 0, **loose))
-    i_mb = done("g", g.iota(T.mb[:], [[0, 8], [1, 16]], 1, 0, **loose))
+    i_strip = done("g", g.iota(T.strip[:], [[1, 144]], 0, 0, **loose))
     for grp, ld, ar in ((diag, "ldD", "aD"), (plane, "ldS", "aS"), (mate, "ldM", "aM")):
         need("g", [(ld, 32)])
         g.remote_dma_fused([RemoteDMATransfer(dst_ids=[dst_id(c)], dma_engine_mask=bits(off[k * half:(k + 1) * half]),
@@ -133,10 +132,16 @@ def rank_program(g, core, T, topo):
     for n, (ca, cb) in enumerate(PIECES):
         j = 16 * ca if n else 0
         i_val.append(done("g", g.iota(T.vals[:, j:16 * cb], [[1, 16 * cb - j]], Z + j, 0, **loose)))
+    i_step = done("g", g.iota(T.step[:], [[0, 2], [1, 16]], 0, 0, **loose))
 
-    need("y", [("sent", 3 * len(off) + len(inner))])
-    for i in range(Q):
-        g.sync.dma_start(T.kvw[:, i * W + Z:(i + 1) * W], T.kv[:, i * M:(i + 1) * M]).then_inc(T.sem.ldkv, 16)
+    me = rank // 2
+    heads = [c for c in diag + plane + mate if R(c) % 2 == rank % 2]
+    order = [None] + [c for c in mate + plane + diag if c in heads]
+    member = lambda c: me if c is None else R(c) // 2
+    need("y", [("sent", 6 * half + len(inner))])
+    for c in order:
+        i = member(c)
+        g.sync.dma_start(T.kvw[:, i * W + Z:(i + 1) * W], T.kv[:, i * M:(i + 1) * M]).then_inc(T.sem["ldk%d" % i], 16)
 
     v, t, s = g.vector, g.tensor, g.scalar
     col = lambda k: T.cst[:, k:k + 1]
@@ -155,7 +160,7 @@ def rank_program(g, core, T, topo):
     x = done("v", v.tensor_scalar(T.bk2[:], T.bm[:], col(1), None, A.mult))
     kb = done("v", v.tensor_scalar(col(3), col(0), -4096.0, 2048.0, A.mult, A.add))
     v_c4 = done("v", v.tensor_scalar(col(4), col(0), float(W), None, A.add))
-    y1 = done("v", v.memset(T.res[:], 1.0))
+    v_res = done("v", v.memset(T.res[:], 1.0))
     need("v", [x])
     ems = [done("v", v.tensor_scalar(T.em[:, blk(k)], T.bk2[:], float(k + 1), None, A.is_equal)) for k in range(16)]
     need("v", [("ldtok", 16)])
@@ -168,16 +173,13 @@ def rank_program(g, core, T, topo):
     need("v", [x2])
     v_lst = done("v", v.tensor_copy(T.lst[:], T.it2[:]))
     v_pars = done("v", v.tensor_scalar(T.pars[:], T.parw[:], col(0), -2048.0, A.subtract, A.add))
-    need("v", [i_mb])
-    x = done("v", v.tensor_tensor(T.bm2[:], T.bm[:], T.mb[:], A.mult))
+    c5 = done("v", v.tensor_scalar(col(5), col(2), 16.0, 15.0, A.mult, A.add))
     v_ones = done("v", v.memset(T.ones[:], 1.0 / 128))
-    need("v", [x, y1])
-    for k in range(16):
-        v_f = done("v", v.tensor_scalar(T.fm[:, blk(k)], T.bm2[:], float(k + 1), -8192.0, A.is_equal, A.mult))
-    v_mask = done("v", v.tensor_scalar(T.mask[:], T.mb[:, 0:32], col(1), 1.0 + 2.0 ** -13, A.is_equal, A.mult))
-    v_res = done("v", v.memset(T.res[:, 16:17], 0.0))
+    need("v", [c5, i_strip])
+    v_f = done("v", v.tensor_scalar(T.fm[:], T.strip[:], col(5), -8192.0, A.is_equal, A.mult))
+    v_f32 = done("v", v.tensor_scalar(T.f32m[:], T.strip[:], col(5), None, A.is_equal))
     for k in range(2):
-        v_o0 = done("v", v.tensor_scalar(T.offw[:, k:k + 1], col(0), float(Z + 16 * k), None, A.add))
+        v_o0 = done("v", v.tensor_scalar(T.offw[:, 30 + k:31 + k], col(0), float(Z + 16 * k), None, A.add))
     for i in range(Q):
         v_kz = done("v", v.memset(T.kvw[:, i * W:i * W + Z], 0.0))
 
@@ -207,7 +209,7 @@ def rank_program(g, core, T, topo):
     done("s", s.activation(T.nxt[:, 0:M], T.ktmp[:], AF.Silu, scale=0.0))
     s_zero = done("s", s.activation(T.nxt[:, M:W], T.ktmp[:, 0:Z], AF.Silu, scale=0.0))
 
-    need("p", [v_ones, i_c16, ks[3]])
+    need("p", [v_ones, v_f, i_c16, ks[3]])
     for n, (ca, cb) in enumerate(PIECES):
         t.matmul(T.psA[:, n * 512:n * 512 + cb - ca], T.ones[:], T.c16[:, ca:cb], True, False)
 
@@ -237,10 +239,10 @@ def rank_program(g, core, T, topo):
         e = done("v", v.tensor_tensor(T.eq[:, 16 * ca:16 * cb], T.tgt[:].indirect(T.lst[:, ca:cb]), T.kk[:, 16 * ca:16 * cb], A.is_equal))
         need("p", [e])
         for k in range(16):
-            ins = t.matmul(T.psA[:, n * 512:n * 512 + cb - ca], T.fm[:, blk(k)], T.eq[:, 16 * ca + k:16 * cb:16], False, k == 15)
+            ins = t.matmul(T.psA[:, n * 512:n * 512 + cb - ca], T.fm[:, 15 - k:143 - k], T.eq[:, 16 * ca + k:16 * cb:16], False, k == 15)
         p_ok.append(done("p", ins))
 
-    scat = []
+    scat = [s_zero]
 
     def place(n):
         ca, cb = PIECES[n]
@@ -248,60 +250,51 @@ def rank_program(g, core, T, topo):
         o = done("v", v.tensor_tensor(T.offt[:, ca:cb], T.psA[:, n * 512:n * 512 + cb - ca], T.pars[:, ca:cb], A.max))
         need("v", [o])
         o = done("v", v.tensor_scalar(T.offu[:, ca:cb], T.offt[:, ca:cb], col(4), None, A.add))
-        need("s", [o, i_val[n], scat[-1] if scat else s_zero])
+        need("s", [o, i_val[n], scat[-1]])
         scat.append(done("s", s.activation(T.nxt[:].indirect(T.offu[:, ca:cb]), T.vals[:, 16 * ca:16 * cb], AF.Silu)))
 
     fit(0)
-    fit(1)
-    place(0)
-    fit(2)
-    place(1)
-    fit(3)
-    place(2)
-    place(3)
+    for n in range(1, len(PIECES)):
+        fit(n)
+        place(n - 1)
+    place(len(PIECES) - 1)
 
-    need("s", [v_f])
-    s_f32 = done("s", s.activation(T.f32m[:], T.fm[:], AF.Copy, scale=-1.0 / 8192))
-    need("v", [i_val[0], v_mask])
+    need("v", [i_step])
+    x = done("v", v.tensor_scalar(T.mask[:], T.step[:], col(0), 1.0 + 2.0 ** -13, A.is_equal, A.mult))
+    need("v", [x])
     v_m0 = done("v", v.tensor_tensor(T.md[:, 0:32], T.mask[:], T.vals[:, 0:32], A.mult))
 
     def collect(d, dep):
-        need("p", [dep, s_f32, v_k])
-        ins = t.matmul(T.psB[:, 0:32], T.f32m[:, blk(d)], T.md[:, 32 * d:32 * d + 32], d == 0, d == D - 1)
+        need("p", [dep, v_f32, v_k])
+        ins = t.matmul(T.psB[:, 0:32], T.f32m[:, 15 - d:143 - d], T.md[:, 32 * d:32 * d + 32], d == 0, d == D - 1)
         return done("p", ins) if d == D - 1 else None
 
     collect(0, v_m0)
     need("v", [scat[-1]])
     for d in range(1, D):
-        x = done("v", v.tensor_tensor(T.md[:, 32 * d:32 * d + 32], T.nxt[:, 0:W].indirect(T.offw[:, 2 * d - 2:2 * d]), T.mask[:], A.mult))
+        x = done("v", v.tensor_tensor(T.md[:, 32 * d:32 * d + 32], T.nxt[:, 0:W].indirect(T.offw[:, 32 * d - 2:32 * d]), T.mask[:], A.mult))
         p_l = collect(d, x)
         if d < D - 1:
             need("v", [x])
-            x = done("v", v.tensor_tensor_scan(T.sc[:, 32 * d:32 * d + 32], T.res[:], T.md[:, 32 * d:32 * d + 32], 0.0, A.mult, A.add))
-            need("v", [x])
-            x = done("v", v.tensor_copy(T.offw[:, 2 * d:2 * d + 2], T.sc[:, 32 * d + 15:32 * d + 32:16]))
+            for h in range(2):
+                x = done("v", v.tensor_tensor_scan(T.offw[:, 32 * d + h:32 * d + 31 + h:2], T.res[:],
+                                                   T.md[:, 32 * d + 16 * h:32 * d + 16 * h + 16], 0.0, A.mult, A.add))
             need("v", [x])
     need("v", [p_l])
     v_lu = done("v", v.tensor_copy(T.lu[:], T.psB[:, 0:32]))
 
-    me = rank // 2
-    heads = [c for c in diag + plane + mate if R(c) % 2 == rank % 2]
     need("g", [v_lu])
     mine = T.lists[:, me * 32:(me + 1) * 32]
     g.remote_dma_fused([RemoteDMATransfer(dst_ids=[dst_id(c) for c in heads], dma_engine_mask=bits(off), remote_sem=T.sem["li%d" % me],
                                           srcs=[T.lu[:]], dsts=[mine for c in heads], alu_op=0)], local_sem=T.sem.lsent)
 
-    order = [None] + [c for c in mate + plane + diag if c in heads]
-    need("v", [("ldkv", 16 * Q), v_lu])
-    need("s", [("ldkv", 16 * Q), v_lu])
-    for n, c in enumerate(order):
-        i = me if c is None else R(c) // 2
+    for c in order:
+        i = member(c)
         win = T.kvw[:, i * W:(i + 1) * W]
         src = T.lu if c is None else T.lists
         b0 = 0 if c is None else 32 * i
-        if c is not None:
-            need("v", [("li%d" % i, len(off))])
-            need("s", [("li%d" % i, len(off))])
+        for q in "vs":
+            need(q, [("ldk%d" % i, 16), v_lu] + ([("li%d" % i, len(off))] if c is not None else []))
         e1 = done("v", v.tensor_copy(T.ysb[:, i * 512:i * 512 + 256], win.indirect(src[:, b0:b0 + 16])))
         e2 = done("s", s.activation(T.ysb[:, i * 512 + 256:(i + 1) * 512], win.indirect(src[:, b0 + 16:b0 + 32]), AF.Copy))
         need("y", [e1, e2])

@@ -2,8 +2,9 @@ from concourse.bass import DstId, RemoteDMATransfer
 from concourse.mybir import AluOpType as A, ActivationFunctionType as AF
 
 M, S, D, Q = 2048, 32, 16, 4
-Z = 64
+Z = 16
 W = M + Z
+H = M // 2
 PIECES = [(2, 16), (16, 48), (48, 80), (80, 128)]
 
 SCRATCH = {
@@ -14,7 +15,6 @@ SCRATCH = {
     "it1": ("sbuf", [128, 128], "int32"),
     "it2": ("sbuf", [128, 128], "int32"),
     "acc": ("sbuf", [128, 128], "int32"),
-    "acc2": ("sbuf", [128, 128], "int32"),
     "tgt": ("sbuf", [128, 128], "int32"),
     "pcol": ("sbuf", [128, 1], "int32"),
     "pa": ("sbuf", [128, 1], "int32"),
@@ -27,7 +27,7 @@ SCRATCH = {
     "bk2": ("sbuf", [128, 128], "float16"),
     "em": ("sbuf", [128, 2048], "float16"),
     "fm": ("sbuf", [128, 144], "bfloat16"),
-    "f32m": ("sbuf", [128, 144], "float32"),
+    "fh": ("sbuf", [128, 144], "float16"),
     "tokh": ("sbuf", [128, 128], "float16"),
     "hiw": ("sbuf", [128, 128], "float16"),
     "lst": ("sbuf", [128, 128], "uint16"),
@@ -35,16 +35,16 @@ SCRATCH = {
     "ktmp": ("sbuf", [128, 2048], "float32"),
     "kk": ("sbuf", [128, 2048], "float32"),
     "eq": ("sbuf", [128, 2048], "bfloat16"),
-    "offt": ("sbuf", [128, 128], "float32"),
     "offu": ("sbuf", [128, 128], "uint16"),
     "vals": ("sbuf", [128, 2048], "float32"),
     "nxt": ("sbuf", [128, W + M], "float32"),
     "c16": ("sbuf", [128, 128], "bfloat16"),
+    "arow": ("sbuf", [128, 128], "bfloat16"),
     "ones": ("sbuf", [128, 128], "bfloat16"),
     "mask": ("sbuf", [128, 32], "float32"),
-    "res": ("sbuf", [128, 16], "float32"),
-    "md": ("sbuf", [128, 32 * D], "float32"),
-    "offw": ("sbuf", [128, 32 * D], "uint16"),
+    "res": ("sbuf", [128, 16], "bfloat16"),
+    "md": ("sbuf", [128, 32 * D], "float16"),
+    "offw": ("sbuf", [128, 32 * D + 32], "uint16"),
     "lu": ("sbuf", [128, 32], "uint16"),
     "lists": ("sbuf", [128, 32 * Q], "uint16"),
     "kvw": ("sbuf", [128, W * Q], "bfloat16"),
@@ -104,34 +104,37 @@ def rank_program(g, core, T, topo):
     blk = lambda k: slice(k * 128, (k + 1) * 128)
     R = T.rank_of
 
-    for grp, sem in ((diag, "ldD"), (plane, "ldS")):
-        for c in grp:
-            g.sync.dma_start(T.dsc[R(c)], piece(R(c))).then_inc(T.sem[sem], 16)
+    stage = lambda q, c, sem: q.dma_start(T.dsc[R(c)], piece(R(c))).then_inc(T.sem[sem], 16)
+    for c in diag:
+        stage(g.sync, c, "ldD")
+    for c in plane:
+        stage(g.sync, c, "ldS")
+    g.sync.dma_start(slot(rank), piece(rank)).then_inc(T.sem.ldO, 16)
+    stage(g.scalar, same[0], "ldP")
     g.scalar.dma_start(T.tokc[:], T.tok[:]).then_inc(T.sem.ldtok, 16)
     g.scalar.dma_start(T.parw[:], T.par[:]).then_inc(T.sem.ldpar, 16)
     for c in mate:
-        g.scalar.dma_start(T.dsc[R(c)], piece(R(c))).then_inc(T.sem.ldM, 16)
-    g.scalar.dma_start(T.dsc[R(same[0])], piece(R(same[0]))).then_inc(T.sem.ldP, 16)
-    g.scalar.dma_start(slot(rank), piece(rank)).then_inc(T.sem.ldO, 16)
+        stage(g.scalar, c, "ldM")
 
     loose = dict(allow_small_or_imprecise_dtypes=True)
     i_p = done("g", g.iota(T.pcol[:], [[1, 1]], 0, 1))
     i_mg = done("g", g.iota(T.mg[:], [[1, 8], [0, 16]], 0, 0, **loose))
     i_strip = done("g", g.iota(T.strip[:], [[1, 144]], 0, 0, **loose))
+    need("g", [("ldP", 16)])
+    g.remote_dma_fused([RemoteDMATransfer(dst_ids=[dst_id(same[0])], dma_engine_mask=bits(inner),
+                                          remote_sem=T.sem.aP, src=T.dsc[R(same[0])], dst=slot(rank))],
+                       local_sem=T.sem.sent)
     for grp, ld, ar in ((diag, "ldD", "aD"), (plane, "ldS", "aS"), (mate, "ldM", "aM")):
         need("g", [(ld, 32)])
         g.remote_dma_fused([RemoteDMATransfer(dst_ids=[dst_id(c)], dma_engine_mask=bits(off[k * half:(k + 1) * half]),
                                               remote_sem=T.sem[ar], src=T.dsc[R(c)], dst=slot(rank))
                             for k, c in enumerate(grp)], local_sem=T.sem.sent)
-    need("g", [("ldP", 16)])
-    g.remote_dma_fused([RemoteDMATransfer(dst_ids=[dst_id(same[0])], dma_engine_mask=bits(inner),
-                                          remote_sem=T.sem.aP, src=T.dsc[R(same[0])], dst=slot(rank))],
-                       local_sem=T.sem.sent)
-    i_c16 = done("g", g.iota(T.c16[:], [[16, 128]], 0, 0, **loose))
+    done("g", g.iota(T.c16[:], [[16, 128]], W, 0, **loose))
+    i_ar = done("g", g.iota(T.arow[:], [[0, 8], [1, 16]], 0, 0, **loose))
     i_val = []
     for n, (ca, cb) in enumerate(PIECES):
         j = 16 * ca if n else 0
-        i_val.append(done("g", g.iota(T.vals[:, j:16 * cb], [[1, 16 * cb - j]], Z + j, 0, **loose)))
+        i_val.append(done("g", g.iota(T.vals[:, j:16 * cb], [[1, 16 * cb - j]], 1 + j, 0, **loose)))
     i_step = done("g", g.iota(T.step[:], [[0, 2], [1, 16]], 0, 0, **loose))
 
     me = rank // 2
@@ -159,10 +162,10 @@ def rank_program(g, core, T, topo):
     need("v", [x])
     x = done("v", v.tensor_scalar(T.bk2[:], T.bm[:], col(1), None, A.mult))
     kb = done("v", v.tensor_scalar(col(3), col(0), -4096.0, 2048.0, A.mult, A.add))
-    v_c4 = done("v", v.tensor_scalar(col(4), col(0), float(W), None, A.add))
-    v_res = done("v", v.memset(T.res[:], 1.0))
+    done("v", v.memset(T.res[:], 1.0))
     need("v", [x])
-    ems = [done("v", v.tensor_scalar(T.em[:, blk(k)], T.bk2[:], float(k + 1), None, A.is_equal)) for k in range(16)]
+    for k in range(16):
+        done("v", v.tensor_scalar(T.em[:, blk(k)], T.bk2[:], float(k + 1), None, A.is_equal))
     need("v", [("ldtok", 16)])
     v_tok = done("v", v.tensor_scalar(T.tokh[:], T.tokc[:], -2048.0, None, A.add))
     need("v", [("ldpar", 16)])
@@ -171,66 +174,82 @@ def rank_program(g, core, T, topo):
     need("v", [x1])
     v_hi = done("v", v.tensor_scalar(T.hiw[:], T.it1[:], 32.0, None, A.mult))
     need("v", [x2])
-    v_lst = done("v", v.tensor_copy(T.lst[:], T.it2[:]))
-    v_pars = done("v", v.tensor_scalar(T.pars[:], T.parw[:], col(0), -2048.0, A.subtract, A.add))
+    done("v", v.tensor_copy(T.lst[:], T.it2[:]))
+    done("v", v.tensor_scalar(T.pars[:], T.parw[:], 1.0, None, A.add))
     c5 = done("v", v.tensor_scalar(col(5), col(2), 16.0, 15.0, A.mult, A.add))
     v_ones = done("v", v.memset(T.ones[:], 1.0 / 128))
     need("v", [c5, i_strip])
     v_f = done("v", v.tensor_scalar(T.fm[:], T.strip[:], col(5), -8192.0, A.is_equal, A.mult))
-    v_f32 = done("v", v.tensor_scalar(T.f32m[:], T.strip[:], col(5), None, A.is_equal))
-    for k in range(2):
-        v_o0 = done("v", v.tensor_scalar(T.offw[:, 30 + k:31 + k], col(0), float(Z + 16 * k), None, A.add))
+    v_fh = done("v", v.tensor_scalar(T.fh[:], T.strip[:], col(5), None, A.is_equal))
+    lcol = lambda d, h: 32 * d + 16 * h + 16
+    last = [done("v", v.tensor_scalar(T.offw[:, lcol(0, h):lcol(0, h) + 1], col(0), float(1 + 16 * h), None, A.add))
+            for h in range(2)]
     for i in range(Q):
-        v_kz = done("v", v.memset(T.kvw[:, i * W:i * W + Z], 0.0))
+        done("v", v.memset(T.kvw[:, i * W:i * W + Z], 0.0))
 
     pa_done, pb_done = [], []
-    need("p", [v_tok])
-    for bank in range(4):
-        for k in range(4 * bank, 4 * bank + 4):
-            ins = t.matmul(T.psA[:, blk(k)], T.em[:, blk(k)], T.tokh[:], True, True)
-        pa_done.append(done("p", ins))
-    need("p", [v_hi])
-    for bank in range(4):
-        for k in range(4 * bank, 4 * bank + 4):
-            ins = t.matmul(T.psB[:, blk(k)], T.em[:, blk(k)], T.hiw[:], True, True)
-        pb_done.append(done("p", ins))
+    for hf in range(2):
+        need("p", [v_tok])
+        for bank in (2 * hf, 2 * hf + 1):
+            for k in range(4 * bank, 4 * bank + 4):
+                ins = t.matmul(T.psA[:, blk(k)], T.em[:, blk(k)], T.tokh[:], True, True)
+            pa_done.append(done("p", ins))
+        need("p", [v_hi])
+        for bank in range(2):
+            for k in range(8 * bank, 8 * bank + 8):
+                o = H * hf + 64 * k
+                ins = t.matmul(T.psB[:, o:o + 64], T.em[:, blk(k)], T.hiw[:, 64 * hf:64 * hf + 64], True, True)
+            pb_done.append(done("p", ins))
 
-    need("s", [kb])
+    need("s", [i_mg])
+    done("s", s.activation(T.nxt[:, M:W], T.mg[:, 0:Z], AF.Silu, scale=0.0))
     ks = []
     for bank in range(4):
-        need("s", [pa_done[bank]])
+        need("s", [pa_done[bank], kb])
         cs = slice(bank * 512, (bank + 1) * 512)
         ks.append(done("s", s.activation(T.ktmp[:, cs], T.psA[:, cs], AF.Identity, bias=col(3), scale=1.0)))
-    need("v", [ks[3]])
-    for k in range(16):
-        need("v", [pb_done[k // 4]])
-        v_k = done("v", v.tensor_tensor(T.kk[:, k:M:16], T.psB[:, blk(k)], T.ktmp[:, k:M:16], A.add))
-    need("s", [ks[3]])
-    done("s", s.activation(T.nxt[:, 0:M], T.ktmp[:], AF.Silu, scale=0.0))
-    s_zero = done("s", s.activation(T.nxt[:, M:W], T.ktmp[:, 0:Z], AF.Silu, scale=0.0))
+    need("s", ks)
+    s_zero = done("s", s.activation(T.nxt[:, 0:M], T.ktmp[:], AF.Identity, scale=0.0))
 
-    need("p", [v_ones, v_f, i_c16, ks[3]])
+    def ksum(hf):
+        out = []
+        need("v", [ks[2 * hf], ks[2 * hf + 1]])
+        for k in range(16):
+            need("v", [pb_done[2 * hf + k // 8]])
+            o, js = H * hf + 64 * k, slice(H * hf + k, H * hf + H, 16)
+            out.append(done("v", v.tensor_tensor(T.kk[:, js], T.psB[:, o:o + 64], T.ktmp[:, js], A.add)))
+        return out
+
+    v_kA = ksum(0)
+
+    need("p", [v_ones, v_f, i_ar] + ks)
     for n, (ca, cb) in enumerate(PIECES):
-        t.matmul(T.psA[:, n * 512:n * 512 + cb - ca], T.ones[:], T.c16[:, ca:cb], True, False)
+        ps = T.psA[:, n * 512:n * 512 + cb - ca]
+        t.matmul(ps, T.ones[:], T.c16[:, ca:cb], True, False)
+        t.matmul(ps, T.arow[:], T.ones[:, 0:cb - ca], False, False)
 
-    m = lambda o, p, q: done("v", v.tensor_tensor(o, p, q, A.max))
-    need("v", [("ldO", 16), ("aD", 2 * half)])
-    x = m(T.acc[:], slot(R(diag[0])), slot(R(diag[1])))
-    need("v", [x])
-    x = m(T.acc[:], T.acc[:], slot(rank))
-    need("v", [("aS", 2 * half)])
-    z = m(T.acc2[:], slot(R(plane[0])), slot(R(plane[1])))
-    need("v", [z])
-    x = m(T.acc[:], T.acc[:], T.acc2[:])
-    need("v", [x, ("aP", len(inner))])
-    x = m(T.acc[:], T.acc[:], slot(R(same[0])))
-    need("v", [("aM", 2 * half)])
-    z = m(T.acc2[:], slot(R(mate[0])), slot(R(mate[1])))
-    need("v", [z])
-    x = m(T.acc[:], T.acc[:], T.acc2[:])
-    need("v", [x])
-    x = done("v", v.tensor_scalar(T.tgt[:], T.acc[:], 4095, None, A.bitwise_and))
-    need("v", [x, v_k])
+    def both(op, deps=((), ())):
+        out = []
+        for h in range(2):
+            need("v", deps[h])
+            out.append([done("v", op(slice(64 * h, 64 * h + 64)))])
+        return out
+
+    def top(o, p, q, deps=((), ())):
+        return both(lambda c: v.tensor_tensor(o(c), p(c), q(c), A.max), deps)
+
+    part = lambda r: (lambda c: T.land[:, r * 128 + c.start:r * 128 + c.stop])
+    acc, full = (lambda c: T.psB[:, 512 + c.start:512 + c.stop]), (lambda c: T.acc[:, c])
+    need("v", [v_kA[9], ("ldO", 16), ("aP", len(inner))])
+    x = top(acc, part(rank), part(R(same[0])))
+    for grp, ar in ((diag, "aD"), (plane, "aS"), (mate, "aM")):
+        if grp is plane:
+            v_k = ksum(1)[-1]
+        need("v", [(ar, 2 * half)])
+        for c in grp:
+            x = top(full if c == mate[-1] else acc, acc, part(R(c)), x)
+    x = both(lambda c: v.tensor_scalar(T.tgt[:, c], T.acc[:, c], 4095, None, A.bitwise_and), x)
+    need("v", x[1] + [v_k])
 
     p_ok = []
 
@@ -247,9 +266,7 @@ def rank_program(g, core, T, topo):
     def place(n):
         ca, cb = PIECES[n]
         need("v", [p_ok[n]])
-        o = done("v", v.tensor_tensor(T.offt[:, ca:cb], T.psA[:, n * 512:n * 512 + cb - ca], T.pars[:, ca:cb], A.max))
-        need("v", [o])
-        o = done("v", v.tensor_scalar(T.offu[:, ca:cb], T.offt[:, ca:cb], col(4), None, A.add))
+        o = done("v", v.tensor_tensor(T.offu[:, ca:cb], T.psA[:, n * 512:n * 512 + cb - ca], T.pars[:, ca:cb], A.max))
         need("s", [o, i_val[n], scat[-1]])
         scat.append(done("s", s.activation(T.nxt[:].indirect(T.offu[:, ca:cb]), T.vals[:, 16 * ca:16 * cb], AF.Silu)))
 
@@ -260,28 +277,33 @@ def rank_program(g, core, T, topo):
     place(len(PIECES) - 1)
 
     need("v", [i_step])
-    x = done("v", v.tensor_scalar(T.mask[:], T.step[:], col(0), 1.0 + 2.0 ** -13, A.is_equal, A.mult))
+    x = done("v", v.tensor_scalar(T.mask[:], T.step[:], col(0), None, A.is_equal))
     need("v", [x])
     v_m0 = done("v", v.tensor_tensor(T.md[:, 0:32], T.mask[:], T.vals[:, 0:32], A.mult))
 
     def collect(d, dep):
-        need("p", [dep, v_f32, v_k])
-        ins = t.matmul(T.psB[:, 0:32], T.f32m[:, 15 - d:143 - d], T.md[:, 32 * d:32 * d + 32], d == 0, d == D - 1)
+        need("p", [dep, v_fh, v_k])
+        ins = t.matmul(T.psB[:, 0:32], T.fh[:, 15 - d:143 - d], T.md[:, 32 * d:32 * d + 32], d == 0, d == D - 1)
         return done("p", ins) if d == D - 1 else None
 
     collect(0, v_m0)
     need("v", [scat[-1]])
     for d in range(1, D):
-        x = done("v", v.tensor_tensor(T.md[:, 32 * d:32 * d + 32], T.nxt[:, 0:W].indirect(T.offw[:, 32 * d - 2:32 * d]), T.mask[:], A.mult))
-        p_l = collect(d, x)
+        xs = []
+        for h in range(2):
+            need("v", [last[h]])
+            b = lcol(d - 1, h)
+            xs.append(done("v", v.tensor_tensor(T.md[:, 32 * d + 16 * h:32 * d + 16 * h + 16],
+                                                T.nxt[:, 0:W].indirect(T.offw[:, b:b + 1]), T.mask[:, 0:16], A.mult)))
+        p_l = collect(d, xs[1])
         if d < D - 1:
-            need("v", [x])
             for h in range(2):
-                x = done("v", v.tensor_tensor_scan(T.offw[:, 32 * d + h:32 * d + 31 + h:2], T.res[:],
-                                                   T.md[:, 32 * d + 16 * h:32 * d + 16 * h + 16], 0.0, A.mult, A.add))
-            need("v", [x])
+                need("v", [xs[h]])
+                b = lcol(d, h)
+                last[h] = done("v", v.tensor_tensor_scan(T.offw[:, b - 15:b + 1], T.res[:],
+                                                         T.md[:, 32 * d + 16 * h:32 * d + 16 * h + 16], 0.0, A.mult, A.add))
     need("v", [p_l])
-    v_lu = done("v", v.tensor_copy(T.lu[:], T.psB[:, 0:32]))
+    v_lu = done("v", v.tensor_scalar(T.lu[:], T.psB[:, 0:32], float(Z - 1), None, A.add))
 
     need("g", [v_lu])
     mine = T.lists[:, me * 32:(me + 1) * 32]

from concourse.bass import DstId, RemoteDMATransfer
from concourse.mybir import AluOpType as A, ActivationFunctionType as AF

M, S, D, Q = 2048, 32, 16, 4
Z = 16
W = M + Z
H = M // 2
PIECES = [(2, 16), (16, 48), (48, 80), (80, 128)]

SCRATCH = {
    "dsc": ("dram", [8, 128, 128], "int32"),
    "land": ("sbuf", [128, 1024], "int32"),
    "parw": ("sbuf", [128, 128], "int32"),
    "tokc": ("sbuf", [128, 128], "int32"),
    "it1": ("sbuf", [128, 128], "int32"),
    "it2": ("sbuf", [128, 128], "int32"),
    "acc": ("sbuf", [128, 128], "int32"),
    "tgt": ("sbuf", [128, 128], "int32"),
    "pcol": ("sbuf", [128, 1], "int32"),
    "pa": ("sbuf", [128, 1], "int32"),
    "pg": ("sbuf", [128, 1], "int32"),
    "cst": ("sbuf", [128, 16], "float32"),
    "mg": ("sbuf", [128, 128], "float32"),
    "strip": ("sbuf", [128, 144], "float32"),
    "step": ("sbuf", [128, 32], "float32"),
    "bm": ("sbuf", [128, 128], "float16"),
    "bk2": ("sbuf", [128, 128], "float16"),
    "em": ("sbuf", [128, 2048], "float16"),
    "fm": ("sbuf", [128, 144], "bfloat16"),
    "fh": ("sbuf", [128, 144], "float16"),
    "tokh": ("sbuf", [128, 128], "float16"),
    "hiw": ("sbuf", [128, 128], "float16"),
    "lst": ("sbuf", [128, 128], "uint16"),
    "pars": ("sbuf", [128, 128], "float32"),
    "ktmp": ("sbuf", [128, 2048], "float32"),
    "kk": ("sbuf", [128, 2048], "float32"),
    "eq": ("sbuf", [128, 2048], "bfloat16"),
    "offu": ("sbuf", [128, 128], "uint16"),
    "vals": ("sbuf", [128, 2048], "float32"),
    "nxt": ("sbuf", [128, W + M], "float32"),
    "c16": ("sbuf", [128, 128], "bfloat16"),
    "arow": ("sbuf", [128, 128], "bfloat16"),
    "ones": ("sbuf", [128, 128], "bfloat16"),
    "mask": ("sbuf", [128, 32], "float32"),
    "res": ("sbuf", [128, 16], "bfloat16"),
    "md": ("sbuf", [128, 32 * D], "float16"),
    "offw": ("sbuf", [128, 32 * D + 32], "uint16"),
    "lu": ("sbuf", [128, 32], "uint16"),
    "lists": ("sbuf", [128, 32 * Q], "uint16"),
    "kvw": ("sbuf", [128, W * Q], "bfloat16"),
    "ysb": ("sbuf", [128, 512 * Q], "bfloat16"),
    "psA": ("psum", [128, 2048], "float32"),
    "psB": ("psum", [128, 2048], "float32"),
}
SEMAPHORES = ["vs", "ss", "ps", "gs", "ldD", "ldS", "ldM", "ldP", "ldO", "ldpar", "ldtok", "ldk0", "ldk1", "ldk2", "ldk3",
              "sent", "aD", "aS", "aM", "aP", "lsent", "li0", "li1", "li2", "li3", "stored"]


def rank_program(g, core, T, topo):
    rank = T.rank_of(core)
    if rank is None:
        return
    eng = {"v": g.vector, "s": g.scalar, "p": g.tensor, "g": g, "y": g.sync}
    semof = {"v": "vs", "s": "ss", "p": "ps", "g": "gs"}
    count = {"v": 0, "s": 0, "p": 0, "g": 0}
    seen = {}

    def need(q, deps):
        for name, val in deps:
            if seen.get((q, name), 0) < val:
                eng[q].wait_ge(T.sem[name], int(val))
                seen[(q, name)] = val

    def done(q, ins):
        count[q] += 1
        ins.then_inc(T.sem[semof[q]], 1)
        return (semof[q], count[q])

    chip = topo.chip(core)
    same, mate, plane, diag = [], [], [], []
    for c in T.cores:
        if c == core:
            continue
        oc = topo.chip(c)
        if oc == chip:
            same.append(c)
        elif topo.mates(chip, oc):
            mate.append(c)
        elif topo.same_plane(chip, oc):
            plane.append(c)
        else:
            diag.append(c)
    off = topo.engines(core, diag[0])
    half = len(off) // 2
    bits = lambda es: sum(1 << e for e in es)
    inner = [e for e in topo.engines(core, same[0]) if e not in off]

    def dst_id(c):
        a = topo.addr(c)
        return DstId(rid=a[0], pnc=a[1])

    slot = lambda r: T.land[:, r * 128:(r + 1) * 128]
    piece = lambda r: T.best[:, r * M:(r + 1) * M]
    blk = lambda k: slice(k * 128, (k + 1) * 128)
    R = T.rank_of

    stage = lambda q, c, sem: q.dma_start(T.dsc[R(c)], piece(R(c))).then_inc(T.sem[sem], 16)
    for c in diag:
        stage(g.sync, c, "ldD")
    for c in plane:
        stage(g.sync, c, "ldS")
    g.sync.dma_start(slot(rank), piece(rank)).then_inc(T.sem.ldO, 16)
    stage(g.scalar, same[0], "ldP")
    g.scalar.dma_start(T.tokc[:], T.tok[:]).then_inc(T.sem.ldtok, 16)
    g.scalar.dma_start(T.parw[:], T.par[:]).then_inc(T.sem.ldpar, 16)
    for c in mate:
        stage(g.scalar, c, "ldM")

    loose = dict(allow_small_or_imprecise_dtypes=True)
    i_p = done("g", g.iota(T.pcol[:], [[1, 1]], 0, 1))
    i_mg = done("g", g.iota(T.mg[:], [[1, 8], [0, 16]], 0, 0, **loose))
    i_strip = done("g", g.iota(T.strip[:], [[1, 144]], 0, 0, **loose))
    need("g", [("ldP", 16)])
    g.remote_dma_fused([RemoteDMATransfer(dst_ids=[dst_id(same[0])], dma_engine_mask=bits(inner),
                                          remote_sem=T.sem.aP, src=T.dsc[R(same[0])], dst=slot(rank))],
                       local_sem=T.sem.sent)
    for grp, ld, ar in ((diag, "ldD", "aD"), (plane, "ldS", "aS"), (mate, "ldM", "aM")):
        need("g", [(ld, 32)])
        g.remote_dma_fused([RemoteDMATransfer(dst_ids=[dst_id(c)], dma_engine_mask=bits(off[k * half:(k + 1) * half]),
                                              remote_sem=T.sem[ar], src=T.dsc[R(c)], dst=slot(rank))
                            for k, c in enumerate(grp)], local_sem=T.sem.sent)
    done("g", g.iota(T.c16[:], [[16, 128]], W, 0, **loose))
    i_ar = done("g", g.iota(T.arow[:], [[0, 8], [1, 16]], 0, 0, **loose))
    i_val = []
    for n, (ca, cb) in enumerate(PIECES):
        j = 16 * ca if n else 0
        i_val.append(done("g", g.iota(T.vals[:, j:16 * cb], [[1, 16 * cb - j]], 1 + j, 0, **loose)))
    i_step = done("g", g.iota(T.step[:], [[0, 2], [1, 16]], 0, 0, **loose))

    me = rank // 2
    heads = [c for c in diag + plane + mate if R(c) % 2 == rank % 2]
    order = [None] + [c for c in mate + plane + diag if c in heads]
    member = lambda c: me if c is None else R(c) // 2
    need("y", [("sent", 6 * half + len(inner))])
    for c in order:
        i = member(c)
        g.sync.dma_start(T.kvw[:, i * W + Z:(i + 1) * W], T.kv[:, i * M:(i + 1) * M]).then_inc(T.sem["ldk%d" % i], 16)

    v, t, s = g.vector, g.tensor, g.scalar
    col = lambda k: T.cst[:, k:k + 1]

    need("v", [i_p])
    b = done("v", v.tensor_scalar(T.pg[:], T.pcol[:], 4, None, A.arith_shift_right))
    a = done("v", v.tensor_scalar(T.pa[:], T.pcol[:], 15, None, A.bitwise_and))
    need("v", [b])
    c0 = done("v", v.tensor_copy(col(2), T.pg[:]))
    need("v", [a])
    done("v", v.tensor_scalar(col(1), T.pa[:], 1.0, None, A.add))
    done("v", v.tensor_copy(col(0), T.pa[:]))
    need("v", [c0, i_mg])
    x = done("v", v.tensor_scalar(T.bm[:], T.mg[:], col(2), None, A.is_equal))
    need("v", [x])
    x = done("v", v.tensor_scalar(T.bk2[:], T.bm[:], col(1), None, A.mult))
    kb = done("v", v.tensor_scalar(col(3), col(0), -4096.0, 2048.0, A.mult, A.add))
    done("v", v.memset(T.res[:], 1.0))
    need("v", [x])
    for k in range(16):
        done("v", v.tensor_scalar(T.em[:, blk(k)], T.bk2[:], float(k + 1), None, A.is_equal))
    need("v", [("ldtok", 16)])
    v_tok = done("v", v.tensor_scalar(T.tokh[:], T.tokc[:], -2048.0, None, A.add))
    need("v", [("ldpar", 16)])
    x1 = done("v", v.tensor_scalar(T.it1[:], T.parw[:], 1920, None, A.bitwise_and))
    x2 = done("v", v.tensor_scalar(T.it2[:], T.parw[:], 127, None, A.bitwise_and))
    need("v", [x1])
    v_hi = done("v", v.tensor_scalar(T.hiw[:], T.it1[:], 32.0, None, A.mult))
    need("v", [x2])
    done("v", v.tensor_copy(T.lst[:], T.it2[:]))
    done("v", v.tensor_scalar(T.pars[:], T.parw[:], 1.0, None, A.add))
    c5 = done("v", v.tensor_scalar(col(5), col(2), 16.0, 15.0, A.mult, A.add))
    v_ones = done("v", v.memset(T.ones[:], 1.0 / 128))
    need("v", [c5, i_strip])
    v_f = done("v", v.tensor_scalar(T.fm[:], T.strip[:], col(5), -8192.0, A.is_equal, A.mult))
    v_fh = done("v", v.tensor_scalar(T.fh[:], T.strip[:], col(5), None, A.is_equal))
    lcol = lambda d, h: 32 * d + 16 * h + 16
    last = [done("v", v.tensor_scalar(T.offw[:, lcol(0, h):lcol(0, h) + 1], col(0), float(1 + 16 * h), None, A.add))
            for h in range(2)]
    for i in range(Q):
        done("v", v.memset(T.kvw[:, i * W:i * W + Z], 0.0))

    pa_done, pb_done = [], []
    for hf in range(2):
        need("p", [v_tok])
        for bank in (2 * hf, 2 * hf + 1):
            for k in range(4 * bank, 4 * bank + 4):
                ins = t.matmul(T.psA[:, blk(k)], T.em[:, blk(k)], T.tokh[:], True, True)
            pa_done.append(done("p", ins))
        need("p", [v_hi])
        for bank in range(2):
            for k in range(8 * bank, 8 * bank + 8):
                o = H * hf + 64 * k
                ins = t.matmul(T.psB[:, o:o + 64], T.em[:, blk(k)], T.hiw[:, 64 * hf:64 * hf + 64], True, True)
            pb_done.append(done("p", ins))

    need("s", [i_mg])
    done("s", s.activation(T.nxt[:, M:W], T.mg[:, 0:Z], AF.Silu, scale=0.0))
    ks = []
    for bank in range(4):
        need("s", [pa_done[bank], kb])
        cs = slice(bank * 512, (bank + 1) * 512)
        ks.append(done("s", s.activation(T.ktmp[:, cs], T.psA[:, cs], AF.Identity, bias=col(3), scale=1.0)))
    need("s", ks)
    s_zero = done("s", s.activation(T.nxt[:, 0:M], T.ktmp[:], AF.Identity, scale=0.0))

    def ksum(hf):
        out = []
        need("v", [ks[2 * hf], ks[2 * hf + 1]])
        for k in range(16):
            need("v", [pb_done[2 * hf + k // 8]])
            o, js = H * hf + 64 * k, slice(H * hf + k, H * hf + H, 16)
            out.append(done("v", v.tensor_tensor(T.kk[:, js], T.psB[:, o:o + 64], T.ktmp[:, js], A.add)))
        return out

    v_kA = ksum(0)

    need("p", [v_ones, v_f, i_ar] + ks)
    for n, (ca, cb) in enumerate(PIECES):
        ps = T.psA[:, n * 512:n * 512 + cb - ca]
        t.matmul(ps, T.ones[:], T.c16[:, ca:cb], True, False)
        t.matmul(ps, T.arow[:], T.ones[:, 0:cb - ca], False, False)

    def both(op, deps=((), ())):
        out = []
        for h in range(2):
            need("v", deps[h])
            out.append([done("v", op(slice(64 * h, 64 * h + 64)))])
        return out

    def top(o, p, q, deps=((), ())):
        return both(lambda c: v.tensor_tensor(o(c), p(c), q(c), A.max), deps)

    part = lambda r: (lambda c: T.land[:, r * 128 + c.start:r * 128 + c.stop])
    acc, full = (lambda c: T.psB[:, 512 + c.start:512 + c.stop]), (lambda c: T.acc[:, c])
    need("v", [v_kA[9], ("ldO", 16), ("aP", len(inner))])
    x = top(acc, part(rank), part(R(same[0])))
    for grp, ar in ((diag, "aD"), (plane, "aS"), (mate, "aM")):
        if grp is plane:
            v_k = ksum(1)[-1]
        need("v", [(ar, 2 * half)])
        for c in grp:
            x = top(full if c == mate[-1] else acc, acc, part(R(c)), x)
    x = both(lambda c: v.tensor_scalar(T.tgt[:, c], T.acc[:, c], 4095, None, A.bitwise_and), x)
    need("v", x[1] + [v_k])

    p_ok = []

    def fit(n):
        ca, cb = PIECES[n]
        e = done("v", v.tensor_tensor(T.eq[:, 16 * ca:16 * cb], T.tgt[:].indirect(T.lst[:, ca:cb]), T.kk[:, 16 * ca:16 * cb], A.is_equal))
        need("p", [e])
        for k in range(16):
            ins = t.matmul(T.psA[:, n * 512:n * 512 + cb - ca], T.fm[:, 15 - k:143 - k], T.eq[:, 16 * ca + k:16 * cb:16], False, k == 15)
        p_ok.append(done("p", ins))

    scat = [s_zero]

    def place(n):
        ca, cb = PIECES[n]
        need("v", [p_ok[n]])
        o = done("v", v.tensor_tensor(T.offu[:, ca:cb], T.psA[:, n * 512:n * 512 + cb - ca], T.pars[:, ca:cb], A.max))
        need("s", [o, i_val[n], scat[-1]])
        scat.append(done("s", s.activation(T.nxt[:].indirect(T.offu[:, ca:cb]), T.vals[:, 16 * ca:16 * cb], AF.Silu)))

    fit(0)
    for n in range(1, len(PIECES)):
        fit(n)
        place(n - 1)
    place(len(PIECES) - 1)

    need("v", [i_step])
    x = done("v", v.tensor_scalar(T.mask[:], T.step[:], col(0), None, A.is_equal))
    need("v", [x])
    v_m0 = done("v", v.tensor_tensor(T.md[:, 0:32], T.mask[:], T.vals[:, 0:32], A.mult))

    def collect(d, dep):
        need("p", [dep, v_fh, v_k])
        ins = t.matmul(T.psB[:, 0:32], T.fh[:, 15 - d:143 - d], T.md[:, 32 * d:32 * d + 32], d == 0, d == D - 1)
        return done("p", ins) if d == D - 1 else None

    collect(0, v_m0)
    need("v", [scat[-1]])
    for d in range(1, D):
        xs = []
        for h in range(2):
            need("v", [last[h]])
            b = lcol(d - 1, h)
            xs.append(done("v", v.tensor_tensor(T.md[:, 32 * d + 16 * h:32 * d + 16 * h + 16],
                                                T.nxt[:, 0:W].indirect(T.offw[:, b:b + 1]), T.mask[:, 0:16], A.mult)))
        p_l = collect(d, xs[1])
        if d < D - 1:
            for h in range(2):
                need("v", [xs[h]])
                b = lcol(d, h)
                last[h] = done("v", v.tensor_tensor_scan(T.offw[:, b - 15:b + 1], T.res[:],
                                                         T.md[:, 32 * d + 16 * h:32 * d + 16 * h + 16], 0.0, A.mult, A.add))
    need("v", [p_l])
    v_lu = done("v", v.tensor_scalar(T.lu[:], T.psB[:, 0:32], float(Z - 1), None, A.add))

    need("g", [v_lu])
    mine = T.lists[:, me * 32:(me + 1) * 32]
    g.remote_dma_fused([RemoteDMATransfer(dst_ids=[dst_id(c) for c in heads], dma_engine_mask=bits(off), remote_sem=T.sem["li%d" % me],
                                          srcs=[T.lu[:]], dsts=[mine for c in heads], alu_op=0)], local_sem=T.sem.lsent)

    for c in order:
        i = member(c)
        win = T.kvw[:, i * W:(i + 1) * W]
        src = T.lu if c is None else T.lists
        b0 = 0 if c is None else 32 * i
        for q in "vs":
            need(q, [("ldk%d" % i, 16), v_lu] + ([("li%d" % i, len(off))] if c is not None else []))
        e1 = done("v", v.tensor_copy(T.ysb[:, i * 512:i * 512 + 256], win.indirect(src[:, b0:b0 + 16])))
        e2 = done("s", s.activation(T.ysb[:, i * 512 + 256:(i + 1) * 512], win.indirect(src[:, b0 + 16:b0 + 32]), AF.Copy))
        need("y", [e1, e2])
        g.sync.dma_start(T.y[:, i * 512:(i + 1) * 512], T.ysb[:, i * 512:(i + 1) * 512]).then_inc(T.sem.stored, 16)
    need("g", [("lsent", len(off)), ("gs", count["g"]), ("ps", count["p"])])
    need("y", [("stored", 16 * Q)])
